import numpy as np
import ml_dtypes


def mxq(x, axis, fmt="e4m3"):
    dtype, down = {"e4m3": (ml_dtypes.float8_e4m3fn, 7), "e5m2": (ml_dtypes.float8_e5m2, 14)}[fmt]
    v = np.moveaxis(np.asarray(x, np.float32).astype(ml_dtypes.bfloat16).astype(np.float64), axis, -1)
    blocks = v.reshape(v.shape[:-1] + (-1, 32))
    amax = np.abs(blocks).max(-1, keepdims=True)
    byte = np.maximum(np.where(amax > 0, np.frexp(amax)[1] - 1 + 127, 0) - down, 1)
    scale = np.exp2(byte - 127.0)
    codes = (blocks / scale).astype(np.float32).astype(dtype).astype(np.float64)
    return np.moveaxis((codes * scale).reshape(v.shape), -1, axis)


WIDE = False


def mx_kscale(k):
    if not WIDE:
        return np.ones(k)
    levels = np.array([10, -10, 5, -5, 0])
    if k % 512:
        return np.exp2(np.random.permutation(np.resize(levels, k // 32))).repeat(32)
    a = np.empty((k // 512, 16))
    for p in range(k // 512):
        a[p, :8] = np.random.permutation(np.resize(levels, 8))
        for g in range(8):
            far = levels[np.abs(levels - a[p, g]) >= 10]
            a[p, g + 8] = far[np.random.randint(len(far))]
    return np.exp2(a.ravel()).repeat(32)


BF16 = ml_dtypes.bfloat16


def bf(x):
    return np.asarray(x, np.float32).astype(BF16)


def f64(x):
    return np.asarray(x).astype(np.float64)

E4M3FN = np.array([(-1.0 if i & 128 else 1.0) * ((1.0 + (i & 7) / 8.0) * 2.0 ** (((i >> 3) & 15) - 7) if i & 120 else (i & 7) * 2.0 ** -9) for i in range(256)])


def e4m3fn_bytes(y):
    return np.clip(np.asarray(y, np.float64), -448.0, 448.0).astype(np.float32).astype(ml_dtypes.float8_e4m3fn).view(np.uint8)


def e4m3fn_values(b):
    return E4M3FN[b]


D, T, R, N = 2048, 1024, 512, 1024


def setup_inputs():
    u = mx_kscale(D)
    v = mx_kscale(R)
    x = np.random.standard_normal((D, T)) * u[:, None]
    b = np.random.standard_normal((R, N)) / np.sqrt(R) / v[:, None]
    x_scale = (np.abs(x).max(axis=1, keepdims=True) / 448.0).astype(np.float32)
    b_scale = (np.abs(b).max(axis=1, keepdims=True) / 448.0).astype(np.float32)
    return {"x_bytes": e4m3fn_bytes(x / f64(x_scale)),
            "x_scale": x_scale,
            "w": bf(np.random.standard_normal((D, N)) / np.sqrt(D) / u[:, None]),
            "a": bf(np.random.standard_normal((D, R)) / np.sqrt(D) / u[:, None] * v),
            "theta": bf(0.5 * np.random.standard_normal(R) * v),
            "b_bytes": e4m3fn_bytes(b / f64(b_scale)),
            "b_scale": b_scale}


def reference(x_bytes, x_scale, w, a, theta, b_bytes, b_scale):
    x = e4m3fn_values(x_bytes) * np.repeat(f64(x_scale), T, axis=1)
    b = e4m3fn_values(b_bytes) * np.repeat(f64(b_scale), N, axis=1)
    xq = mxq(x, 0, "e4m3")
    y = xq.T @ mxq(f64(w), 0, "e4m3")
    c = xq.T @ mxq(f64(a), 0, "e4m3")
    h = np.maximum(c - f64(theta), 0.0)
    r = mxq(h, 1, "e4m3") @ mxq(b, 0, "e4m3")
    return y - r

@@ -1,0 +1,301 @@
+from contextlib import ExitStack
+
+import concourse.mybir as mybir
+
+D, T, R, N = 2048, 1024, 512, 1024
+
+F32 = mybir.dt.float32
+BF16 = mybir.dt.bfloat16
+U32 = mybir.dt.uint32
+U8 = mybir.dt.uint8
+FP8 = mybir.dt.float8_e4m3fn
+FP8X4 = mybir.dt.float8_e4m3fn_x4
+ACT = mybir.ActivationFunctionType
+ALU = mybir.AluOpType
+
+FLOPS = 2 * T * D * (R + N) + 2 * T * R * N
+
+P = 128
+G = D // 512
+HALF = 512
+RUN = 4
+
+
+def tile_steering_directions_out_d5_kernel(tc, x_bytes, x_scale, w, a, theta, b_bytes, b_scale, out):
+    nc = tc.nc
+    with ExitStack() as ctx:
+        keep = ctx.enter_context(tc.tile_pool(name="keep", bufs=1))
+        stage = ctx.enter_context(tc.tile_pool(name="stage", bufs=8))
+        outs = ctx.enter_context(tc.tile_pool(name="outs", bufs=8))
+        psum = ctx.enter_context(tc.psum_pool(name="psum", bufs=1))
+        ctx.enter_context(tc.manual_schedule())
+
+        def kept(name, shape, dtype):
+            return keep.tile(shape, dtype, name=name, align_bytes=64)
+
+        theta_bf = kept("theta_bf", [P, 4], BF16)
+        b_s = kept("b_s", [P, 4], F32)
+        x_s = kept("x_s", [P, 4 * G], F32)
+        neg_theta = kept("neg_theta", [P, 4], F32)
+        neg_b_s = kept("neg_b_s", [P, 4], F32)
+
+        a_raw, x_raw, w_raw = {}, {}, {}
+        for g in range(G):
+            a_raw[g] = kept("a_raw%d" % g, [P, 4, R], BF16)
+            for half in range(2):
+                x_raw[(g, half)] = kept("x_raw%d%d" % (g, half), [P, 4, HALF], U8)
+                w_raw[(g, half)] = kept("w_raw%d%d" % (g, half), [P, 4, HALF], BF16)
+        b_raw = kept("b_raw", [P, 4, N], U8)
+
+        def rows(src, g):
+            return src[512 * g : 512 * (g + 1), :].rearrange("(p t) c -> p t c", t=4)
+
+        def load_small():
+            nc.scalar.dma_start(out=x_s[:].rearrange("p (g t) -> p g t", t=4), in_=x_scale.rearrange("(g p t) o -> p g (t o)", p=P, t=4))
+            nc.scalar.dma_start(out=theta_bf[:], in_=theta.rearrange("(p t) -> p t", t=4))
+            nc.scalar.dma_start(out=b_s[:], in_=b_scale.rearrange("(p t) o -> p (t o)", t=4))
+
+        def load(key):
+            g, half = int(key[1]) if len(key) > 1 else 0, int(key[-1]) if len(key) > 2 else 0
+            cols = slice(half * HALF, (half + 1) * HALF)
+            if key[0] == "a":
+                nc.sync.dma_start(out=a_raw[g][:], in_=rows(a, g))
+            elif key[0] == "b":
+                nc.sync.dma_start(out=b_raw[:], in_=rows(b_bytes, 0))
+            elif key[0] == "x":
+                nc.sync.dma_start(out=x_raw[(g, half)][:], in_=rows(x_bytes, g)[:, :, cols])
+            else:
+                nc.sync.dma_start(out=w_raw[(g, half)][:], in_=rows(w, g)[:, :, cols])
+
+        wide, codes, scales, grouped, banks, h_raw = {}, {}, {}, {}, {}, {}
+
+        def op_negate():
+            nc.scalar.mul(out=neg_theta[:], in_=theta_bf[:], mul=-1.0)
+            nc.scalar.mul(out=neg_b_s[:], in_=b_s[:], mul=-1.0)
+
+        def op_wide(eng, key, t0=0, t1=4):
+            i, half = int(key[1]), int(key[-1])
+            if key[0] == "x":
+                raw, col, sc = x_raw[(i, half)], 0, x_s[:, 4 * i : 4 * i + 4]
+            else:
+                raw, col, sc = b_raw, half * HALF, neg_b_s[:]
+            if key not in wide:
+                wide[key] = stage.tile([P, 4, HALF], BF16, name="wide", align_bytes=64)
+            for t in range(t0, t1):
+                view = raw[:, t, col : col + HALF].bitcast(FP8)
+                if eng == "S":
+                    nc.scalar.activation(out=wide[key][:, t, :], in_=view, func=ACT.Copy, scale=sc[:, t : t + 1])
+                else:
+                    nc.vector.tensor_scalar(out=wide[key][:, t, :], in0=view, scalar1=sc[:, t : t + 1], scalar2=None, op0=ALU.mult)
+
+        def source(key):
+            if key[0] == "a":
+                return a_raw[int(key[1])][:]
+            if key[0] == "w":
+                return w_raw[(int(key[1]), int(key[2]))][:]
+            if key[0] == "h":
+                return h_raw[int(key[1])][:]
+            return wide[key][:]
+
+        def views(key, n0, n1):
+            src = source(key)
+            if key[0] == "a":
+                dst = grouped[key][:].rearrange("p (t m j) -> p m j t", t=4, j=4)
+                return dst[:, n0 // 4 : n1 // 4], src.rearrange("p j (m t) -> p m j t", t=4)[:, n0 // 4 : n1 // 4]
+            dst = grouped[key][:].rearrange("p (c i t) -> p c t i", i=RUN, t=4)
+            return dst[:, n0 // RUN : n1 // RUN], src.rearrange("p t (c i) -> p c t i", i=RUN)[:, n0 // RUN : n1 // RUN]
+
+        def new_grouped(eng, key):
+            grouped[key] = stage.tile([P, 4 * HALF], BF16, name="grouped", align_bytes=64)
+
+        def op_inter(eng, key, n0=0, n1=HALF):
+            if key not in grouped:
+                new_grouped(eng, key)
+            dst, src = views(key, n0, n1)
+            if eng == "V":
+                nc.vector.tensor_copy(out=dst, in_=src)
+            else:
+                nc.scalar.copy(out=dst, in_=src)
+
+        def op_quant(eng, key):
+            codes[key] = kept("codes_" + key, [P, HALF], U32)
+            scales[key] = kept("scales_" + key, [P, HALF], U8)
+            nc.vector.quantize_mx(out=codes[key][:].bitcast(FP8X4), scales=scales[key][:], in_=grouped[key][:])
+
+        def multiply(bank, stat, block, mov, start, stop):
+            cols = slice(block * P, (block + 1) * P)
+            nc.tensor.matmul_mx(
+                out=bank[:],
+                lhsT=codes[stat][:, cols].bitcast(FP8X4),
+                lhsT_scale=scales[stat][:, cols],
+                rhs=codes[mov][:].bitcast(FP8X4),
+                rhs_scale=scales[mov][:],
+                start=start,
+                stop=stop,
+            )
+
+        def bank_tile(i):
+            return psum.tile([P, HALF], F32, name="bank%d" % i)
+
+        def op_c(eng, g, th, t, start, stop):
+            if start:
+                banks[("c", th, t)] = bank_tile(4 * th + t)
+            multiply(banks[("c", th, t)], "a%d" % g, t, "x%d%d" % (g, th), start, stop)
+
+        def op_cexit(eng, th, t):
+            if th not in h_raw:
+                h_raw[th] = kept("h_raw%d" % th, [P, 4, HALF], BF16)
+            if eng == "S":
+                nc.scalar.activation(out=h_raw[th][:, t, :], in_=banks[("c", th, t)][:], func=ACT.Relu, bias=neg_theta[:, t : t + 1])
+            else:
+                nc.vector.tensor_scalar(
+                    out=h_raw[th][:, t, :], in0=banks[("c", th, t)][:], scalar1=neg_theta[:, t : t + 1], scalar2=0.0, op0=ALU.add, op1=ALU.max
+                )
+
+        def op_y(eng, nh, i, g, start, stop):
+            if start:
+                banks[("y", nh, i)] = bank_tile(i)
+            if g == "r":
+                multiply(banks[("y", nh, i)], "h%d" % (i // 4), i % 4, "b%d" % nh, start, stop)
+            else:
+                multiply(banks[("y", nh, i)], "x%d%d" % (g, i // 4), i % 4, "w%d%d" % (g, nh), start, stop)
+
+        def op_yexit(eng, nh, i):
+            o = outs.tile([P, HALF], F32, name="o")
+            if eng == "V":
+                nc.vector.tensor_copy(out=o[:], in_=banks[("y", nh, i)][:])
+            else:
+                nc.scalar.copy(out=o[:], in_=banks[("y", nh, i)][:])
+            nc.sync.dma_start(out=out[i * P : (i + 1) * P, nh * HALF : (nh + 1) * HALF], in_=o[:])
+
+        ops = {"wide": op_wide, "inter": op_inter, "quant": op_quant, "c": op_c, "cexit": op_cexit, "y": op_y, "yexit": op_yexit}
+
+        def needs(step):
+            op, args = step[0], step[1:]
+            if op == "wide":
+                return []
+            if op == "inter":
+                key = args[0]
+                if key[0] in "xb":
+                    return [s for s in all_steps if s[0] == "wide" and s[1] == key]
+                if key[0] == "h":
+                    return [("cexit", int(key[1]), t) for t in range(4)]
+                return []
+            if op == "quant":
+                return [s for s in all_steps if s[0] == "inter" and s[1] == args[0]]
+            if op == "c":
+                g, th, t, start, stop = args
+                found = [("quant", "a%d" % g), ("quant", "x%d%d" % (g, th))]
+                return found
+            if op == "cexit":
+                return [s for s in all_steps if s[0] == "c" and s[2:4] == args]
+            if op == "y":
+                nh, i, g, start, stop = args
+                keys = ["h%d" % (i // 4), "b%d" % nh] if g == "r" else ["x%d%d" % (g, i // 4), "w%d%d" % (g, nh)]
+                found = [("quant", k) for k in keys]
+                if start:
+                    found.append(("cexit", i // 4, i % 4) if nh == 0 else ("yexit", 0, i))
+                return found
+            if op == "yexit":
+                return [s for s in all_steps if s[0] == "y" and s[1:3] == args]
+
+        def loads():
+            for key in ["x00","a0","x10","a1","x20","a2","x30","a3","x01","w00","x11","w10","x21","w20","x31","w30","b","w01","w11","w21","w31"]:
+                load(key)
+
+        pairs = [["a0","x00"],["a1","x10"],["a3","x20"],["x30","a2"],["x11","x31"],["x01","x21"],["w10","w20"],["h0","w00"],["b0","w30"],["h1","w31"],["b1","w21"],["w11","w01"]]
+        vector_wide = {"x00":0,"x10":0,"x21":1,"b1":1}
+        scalar_inter = {"x01":1,"h1":0,"w01":0,"w11":0,"w20":0,"w21":0,"w30":0,"a3":3}
+        v_list, s_list, t_list = [], [], []
+
+        def wide_steps(key, by_vector):
+            if key[0] not in "xb":
+                return []
+            return [("wide", key, 2 * h, 2 * h + 2) for h in range(2) if (vector_wide.get(key, 2) in (h, 3)) == by_vector]
+
+        def inter_steps(key, by_vector):
+            hh = [h for h in range(2) if (scalar_inter.get(key, 2) in (h, 3)) != by_vector]
+            if len(hh) == 2:
+                return [("inter", key, 0, HALF)]
+            return [("inter", key, h * HALF // 2, (h + 1) * HALF // 2) for h in hh]
+
+        for n, pair in enumerate(pairs):
+            for key in pair:
+                v_list += wide_steps(key, True)
+                s_list += wide_steps(key, False)
+            for key in pair:
+                v_list += inter_steps(key, True)
+                s_list += inter_steps(key, False)
+            v_list += [("quant", key) for key in pair]
+            if n == 6:
+                s_list += [("cexit", 0, t) for t in range(4)]
+            if n == 6:
+                s_list += [("cexit", 1, t) for t in range(4)]
+            if n == 10:
+                s_list += [("yexit", 0, i) for i in range(4)]
+            if n == 10:
+                s_list += [("yexit", 0, i) for i in range(4, 8)]
+        v_list += [("yexit", 1, i) for i in range(8) if i in [0,1,2,3,4,5]]
+        s_list += [("yexit", 1, i) for i in range(8) if i not in [0,1,2,3,4,5]]
+
+        runs = [("c", g, th, 0) for th in range(2) for g in range(G)]
+        runs += [("y", g, th, nh) for nh in range(2) for th in range(2) for g in (0, 1, 2, 3, "r")]
+        last_w = [int(key[1]) for pair in pairs for key in pair if key[0] == "w" and key[2] == "1"][2:]
+        ready, written = [], []
+
+        def operands(run):
+            kind, g, th, nh = run
+            if kind == "c":
+                return ["a%d" % g, "x%d%d" % (g, th)]
+            return ["h%d" % th, "b%d" % nh] if g == "r" else ["x%d%d" % (g, th), "w%d%d" % (g, nh)]
+
+        def can(run):
+            kind, g, th, nh = run
+            if run in written or not all(key in ready for key in operands(run)):
+                return False
+            if kind == "c":
+                return True
+            if nh == 0:
+                return all(r in written for r in runs if r[0] == "c" and r[2] == th)
+            return g not in last_w and all(r in written for r in runs if r[0] == "y" and r[2] == th and r[3] == 0)
+
+        for pair in pairs:
+            for key in pair:
+                ready.append(key)
+                for again in range(2):
+                    for run in [r for r in runs if can(r)]:
+                        written.append(run)
+        passes = []
+        for kind, g, th, nh in written:
+            for i in range(4):
+                passes.append(("c", g, th, i) if kind == "c" else ("y", nh, 4 * th + i, g))
+        for i in range(8):
+            for kind, g, th, nh in runs:
+                if (kind, g, th, nh) not in written and th == i // 4:
+                    passes.append(("y", nh, i, g))
+
+        def group(step):
+            return step[:1] + step[2:] if step[0] == "c" else step[:3]
+
+        for n, step in enumerate(passes):
+            start = all(group(s) != group(step) for s in passes[:n])
+            stop = all(group(s) != group(step) for s in passes[n + 1 :])
+            t_list.append(step + (start, stop))
+
+        queues = {"S": s_list, "V": v_list, "T": t_list}
+        all_steps = s_list + v_list + t_list
+        done = set()
+        load_small()
+        loads()
+        op_negate()
+        while any(queues.values()):
+            before = len(done)
+            for eng in ("T", "V", "S"):
+                while queues[eng] and all(s in done for s in needs(queues[eng][0])):
+                    step = queues[eng][0]
+                    queues[eng] = queues[eng][1:]
+                    ops[step[0]](eng, *step[1:])
+                    done.add(step)
+                    if eng == "S":
+                        break
+            assert len(done) > before

@@ -18,6 +18,7 @@ FLOPS = 2 * T * D * (R + N) + 2 * T * R * N
 P = 128
 G = D // 512
 HALF = 512
+TILES = T // P
 RUN = 4
 
 
@@ -35,259 +36,235 @@ def tile_steering_directions_out_d5_kernel(tc, x_bytes, x_scale, w, a, theta, b_
 
         theta_bf = kept("theta_bf", [P, 4], BF16)
         b_s = kept("b_s", [P, 4], F32)
-        x_s = kept("x_s", [P, 4 * G], F32)
         neg_theta = kept("neg_theta", [P, 4], F32)
         neg_b_s = kept("neg_b_s", [P, 4], F32)
-
-        a_raw, x_raw, w_raw = {}, {}, {}
+        x_s, raw = {}, {}
         for g in range(G):
-            a_raw[g] = kept("a_raw%d" % g, [P, 4, R], BF16)
-            for half in range(2):
-                x_raw[(g, half)] = kept("x_raw%d%d" % (g, half), [P, 4, HALF], U8)
-                w_raw[(g, half)] = kept("w_raw%d%d" % (g, half), [P, 4, HALF], BF16)
-        b_raw = kept("b_raw", [P, 4, N], U8)
+            x_s[g] = kept("x_s%d" % g, [P, 4], F32)
 
         def rows(src, g):
             return src[512 * g : 512 * (g + 1), :].rearrange("(p t) c -> p t c", t=4)
 
-        def load_small():
-            nc.scalar.dma_start(out=x_s[:].rearrange("p (g t) -> p g t", t=4), in_=x_scale.rearrange("(g p t) o -> p g (t o)", p=P, t=4))
-            nc.scalar.dma_start(out=theta_bf[:], in_=theta.rearrange("(p t) -> p t", t=4))
-            nc.scalar.dma_start(out=b_s[:], in_=b_scale.rearrange("(p t) o -> p (t o)", t=4))
-
         def load(key):
-            g, half = int(key[1]) if len(key) > 1 else 0, int(key[-1]) if len(key) > 2 else 0
-            cols = slice(half * HALF, (half + 1) * HALF)
-            if key[0] == "a":
-                nc.sync.dma_start(out=a_raw[g][:], in_=rows(a, g))
-            elif key[0] == "b":
-                nc.sync.dma_start(out=b_raw[:], in_=rows(b_bytes, 0))
-            elif key[0] == "x":
-                nc.sync.dma_start(out=x_raw[(g, half)][:], in_=rows(x_bytes, g)[:, :, cols])
-            else:
-                nc.sync.dma_start(out=w_raw[(g, half)][:], in_=rows(w, g)[:, :, cols])
+            if key == "vectors":
+                nc.sync.dma_start(out=theta_bf[:], in_=theta.rearrange("(p t) -> p t", t=4))
+                nc.sync.dma_start(out=b_s[:], in_=rows(b_scale, 0).rearrange("p t o -> p (t o)"))
+                return
+            if key[0] == "s":
+                g = int(key[1])
+                queue = nc.scalar if g == 0 else nc.sync
+                queue.dma_start(out=x_s[g][:], in_=rows(x_scale, g).rearrange("p t o -> p (t o)"))
+                return
+            kind, g = key[0], int(key[1]) if len(key) > 1 else 0
+            src = {"a": a, "b": b_bytes, "x": x_bytes, "w": w}[kind]
+            width = N if kind == "b" else HALF
+            c0 = int(key[2]) * HALF if len(key) > 2 else 0
+            raw[key] = kept("raw_" + key, [P, 4, width], U8 if kind in "xb" else BF16)
+            nc.sync.dma_start(out=raw[key][:], in_=rows(src, g)[:, :, c0 : c0 + width])
 
         wide, codes, scales, grouped, banks, h_raw = {}, {}, {}, {}, {}, {}
 
-        def op_negate():
+        def op_negate(eng):
             nc.scalar.mul(out=neg_theta[:], in_=theta_bf[:], mul=-1.0)
             nc.scalar.mul(out=neg_b_s[:], in_=b_s[:], mul=-1.0)
 
-        def op_wide(eng, key, t0=0, t1=4):
-            i, half = int(key[1]), int(key[-1])
-            if key[0] == "x":
-                raw, col, sc = x_raw[(i, half)], 0, x_s[:, 4 * i : 4 * i + 4]
-            else:
-                raw, col, sc = b_raw, half * HALF, neg_b_s[:]
+        def op_widen(eng, key, planes):
             if key not in wide:
                 wide[key] = stage.tile([P, 4, HALF], BF16, name="wide", align_bytes=64)
-            for t in range(t0, t1):
-                view = raw[:, t, col : col + HALF].bitcast(FP8)
-                if eng == "S":
-                    nc.scalar.activation(out=wide[key][:, t, :], in_=view, func=ACT.Copy, scale=sc[:, t : t + 1])
+            for t in planes:
+                if key[0] == "x":
+                    view, scale = raw[key][:, t, :], x_s[int(key[1])][:, t : t + 1]
                 else:
-                    nc.vector.tensor_scalar(out=wide[key][:, t, :], in0=view, scalar1=sc[:, t : t + 1], scalar2=None, op0=ALU.mult)
+                    c0 = int(key[1]) * HALF
+                    view, scale = raw["b"][:, t, c0 : c0 + HALF], neg_b_s[:, t : t + 1]
+                if eng == "S":
+                    nc.scalar.activation(out=wide[key][:, t, :], in_=view.bitcast(FP8), func=ACT.Copy, scale=scale)
+                else:
+                    nc.vector.tensor_scalar(out=wide[key][:, t, :], in0=view.bitcast(FP8), scalar1=scale, scalar2=None, op0=ALU.mult)
 
-        def source(key):
-            if key[0] == "a":
-                return a_raw[int(key[1])][:]
-            if key[0] == "w":
-                return w_raw[(int(key[1]), int(key[2]))][:]
-            if key[0] == "h":
-                return h_raw[int(key[1])][:]
-            return wide[key][:]
-
-        def views(key, n0, n1):
-            src = source(key)
+        def op_lay(eng, key, half):
+            if key not in grouped:
+                grouped[key] = stage.tile([P, 4 * HALF], BF16, name="grouped", align_bytes=64)
+            src = {"a": raw, "w": raw, "x": wide, "b": wide, "h": h_raw}[key[0]][key][:]
             if key[0] == "a":
                 dst = grouped[key][:].rearrange("p (t m j) -> p m j t", t=4, j=4)
-                return dst[:, n0 // 4 : n1 // 4], src.rearrange("p j (m t) -> p m j t", t=4)[:, n0 // 4 : n1 // 4]
-            dst = grouped[key][:].rearrange("p (c i t) -> p c t i", i=RUN, t=4)
-            return dst[:, n0 // RUN : n1 // RUN], src.rearrange("p t (c i) -> p c t i", i=RUN)[:, n0 // RUN : n1 // RUN]
-
-        def new_grouped(eng, key):
-            grouped[key] = stage.tile([P, 4 * HALF], BF16, name="grouped", align_bytes=64)
-
-        def op_inter(eng, key, n0=0, n1=HALF):
-            if key not in grouped:
-                new_grouped(eng, key)
-            dst, src = views(key, n0, n1)
-            if eng == "V":
-                nc.vector.tensor_copy(out=dst, in_=src)
+                src = src.rearrange("p j (m t) -> p m j t", t=4)
             else:
-                nc.scalar.copy(out=dst, in_=src)
+                dst = grouped[key][:].rearrange("p (c i t) -> p c t i", i=RUN, t=4)
+                src = src.rearrange("p t (c i) -> p c t i", i=RUN)
+            count = src.shape[1]
+            part = {0: slice(0, count // 2), 1: slice(count // 2, count), None: slice(0, count)}[half]
+            if eng == "V":
+                nc.vector.tensor_copy(out=dst[:, part], in_=src[:, part])
+            else:
+                nc.scalar.copy(out=dst[:, part], in_=src[:, part])
 
-        def op_quant(eng, key):
+        def op_quantize(eng, key):
             codes[key] = kept("codes_" + key, [P, HALF], U32)
             scales[key] = kept("scales_" + key, [P, HALF], U8)
             nc.vector.quantize_mx(out=codes[key][:].bitcast(FP8X4), scales=scales[key][:], in_=grouped[key][:])
 
-        def multiply(bank, stat, block, mov, start, stop):
-            cols = slice(block * P, (block + 1) * P)
+        def multiply(bank, stat, block, mov, cols, start, stop):
+            mine = slice(block * P, (block + 1) * P)
             nc.tensor.matmul_mx(
-                out=bank[:],
-                lhsT=codes[stat][:, cols].bitcast(FP8X4),
-                lhsT_scale=scales[stat][:, cols],
-                rhs=codes[mov][:].bitcast(FP8X4),
-                rhs_scale=scales[mov][:],
+                out=bank[:, 0 : cols.stop - cols.start],
+                lhsT=codes[stat][:, mine].bitcast(FP8X4),
+                lhsT_scale=scales[stat][:, mine],
+                rhs=codes[mov][:, cols].bitcast(FP8X4),
+                rhs_scale=scales[mov][:, cols],
                 start=start,
                 stop=stop,
             )
 
-        def bank_tile(i):
-            return psum.tile([P, HALF], F32, name="bank%d" % i)
+        ALL = slice(0, HALF)
+        blocks = [(nh, i, ALL, i) for nh in range(2) for i in range(TILES)]
+        if True:
+            blocks[-1:] = [(1, 7, slice(0, 256), 7), (1, 7, slice(256, 512), 0)]
 
-        def op_c(eng, g, th, t, start, stop):
+        def new_bank(group, i):
+            banks[group] = psum.tile([P, HALF], F32, name="bank%d" % i)
+
+        def op_c(eng, th, t, g, start, stop):
             if start:
-                banks[("c", th, t)] = bank_tile(4 * th + t)
-            multiply(banks[("c", th, t)], "a%d" % g, t, "x%d%d" % (g, th), start, stop)
+                new_bank(("c", th, t), 4 * th + t)
+            multiply(banks[("c", th, t)], "a%d" % g, t, "x%d%d" % (g, th), ALL, start, stop)
 
-        def op_cexit(eng, th, t):
-            if th not in h_raw:
-                h_raw[th] = kept("h_raw%d" % th, [P, 4, HALF], BF16)
+        def op_relu(eng, th, t):
+            if "h%d" % th not in h_raw:
+                h_raw["h%d" % th] = kept("raw_h%d" % th, [P, 4, HALF], BF16)
+            dst = h_raw["h%d" % th][:, t, :]
             if eng == "S":
-                nc.scalar.activation(out=h_raw[th][:, t, :], in_=banks[("c", th, t)][:], func=ACT.Relu, bias=neg_theta[:, t : t + 1])
+                nc.scalar.activation(out=dst, in_=banks[("c", th, t)][:], func=ACT.Relu, bias=neg_theta[:, t : t + 1])
             else:
-                nc.vector.tensor_scalar(
-                    out=h_raw[th][:, t, :], in0=banks[("c", th, t)][:], scalar1=neg_theta[:, t : t + 1], scalar2=0.0, op0=ALU.add, op1=ALU.max
-                )
+                nc.vector.tensor_scalar(out=dst, in0=banks[("c", th, t)][:], scalar1=neg_theta[:, t : t + 1], scalar2=0.0, op0=ALU.add, op1=ALU.max)
 
-        def op_y(eng, nh, i, g, start, stop):
+        def op_y(eng, n, g, start, stop):
+            nh, i, cols, bank = blocks[n]
             if start:
-                banks[("y", nh, i)] = bank_tile(i)
-            if g == "r":
-                multiply(banks[("y", nh, i)], "h%d" % (i // 4), i % 4, "b%d" % nh, start, stop)
-            else:
-                multiply(banks[("y", nh, i)], "x%d%d" % (g, i // 4), i % 4, "w%d%d" % (g, nh), start, stop)
+                new_bank(("y", n), bank)
+            stat, mov = ("h%d" % (i // 4), "b%d" % nh) if g == "r" else ("x%d%d" % (g, i // 4), "w%d%d" % (g, nh))
+            multiply(banks[("y", n)], stat, i % 4, mov, cols, start, stop)
 
-        def op_yexit(eng, nh, i):
+        def op_store(eng, n):
+            nh, i, cols, bank = blocks[n]
+            width = cols.stop - cols.start
             o = outs.tile([P, HALF], F32, name="o")
             if eng == "V":
-                nc.vector.tensor_copy(out=o[:], in_=banks[("y", nh, i)][:])
+                nc.vector.tensor_copy(out=o[:, 0:width], in_=banks[("y", n)][:, 0:width])
             else:
-                nc.scalar.copy(out=o[:], in_=banks[("y", nh, i)][:])
-            nc.sync.dma_start(out=out[i * P : (i + 1) * P, nh * HALF : (nh + 1) * HALF], in_=o[:])
+                nc.scalar.copy(out=o[:, 0:width], in_=banks[("y", n)][:, 0:width])
+            nc.sync.dma_start(out=out[i * P : (i + 1) * P, nh * HALF + cols.start : nh * HALF + cols.stop], in_=o[:, 0:width])
 
-        ops = {"wide": op_wide, "inter": op_inter, "quant": op_quant, "c": op_c, "cexit": op_cexit, "y": op_y, "yexit": op_yexit}
-
-        def needs(step):
-            op, args = step[0], step[1:]
-            if op == "wide":
-                return []
-            if op == "inter":
-                key = args[0]
-                if key[0] in "xb":
-                    return [s for s in all_steps if s[0] == "wide" and s[1] == key]
-                if key[0] == "h":
-                    return [("cexit", int(key[1]), t) for t in range(4)]
-                return []
-            if op == "quant":
-                return [s for s in all_steps if s[0] == "inter" and s[1] == args[0]]
-            if op == "c":
-                g, th, t, start, stop = args
-                found = [("quant", "a%d" % g), ("quant", "x%d%d" % (g, th))]
-                return found
-            if op == "cexit":
-                return [s for s in all_steps if s[0] == "c" and s[2:4] == args]
-            if op == "y":
-                nh, i, g, start, stop = args
-                keys = ["h%d" % (i // 4), "b%d" % nh] if g == "r" else ["x%d%d" % (g, i // 4), "w%d%d" % (g, nh)]
-                found = [("quant", k) for k in keys]
-                if start:
-                    found.append(("cexit", i // 4, i % 4) if nh == 0 else ("yexit", 0, i))
-                return found
-            if op == "yexit":
-                return [s for s in all_steps if s[0] == "y" and s[1:3] == args]
-
-        def loads():
-            for key in ["x00","a0","x10","a1","x20","a2","x30","a3","x01","w00","x11","w10","x21","w20","x31","w30","b","w01","w11","w21","w31"]:
-                load(key)
+        ops = {"negate": op_negate, "widen": op_widen, "lay": op_lay, "quantize": op_quantize, "c": op_c, "relu": op_relu, "y": op_y, "store": op_store}
 
         pairs = [["a0","x00"],["a1","x10"],["a3","x20"],["x30","a2"],["x11","x31"],["x01","x21"],["w10","w20"],["h0","w00"],["b0","w30"],["h1","w31"],["b1","w21"],["w11","w01"]]
-        vector_wide = {"x00":0,"x10":0,"x21":1,"b1":1}
-        scalar_inter = {"x01":1,"h1":0,"w01":0,"w11":0,"w20":0,"w21":0,"w30":0,"a3":3}
+        vector_widens = {"x00":[0],"x10":[0],"x21":[1],"b1":[1]}
+        scalar_lays = {"x01":[1],"h1":[0],"w01":[0],"w11":[0],"w20":[0],"w21":[0],"w30":[0],"a3":[0,1]}
         v_list, s_list, t_list = [], [], []
-
-        def wide_steps(key, by_vector):
-            if key[0] not in "xb":
-                return []
-            return [("wide", key, 2 * h, 2 * h + 2) for h in range(2) if (vector_wide.get(key, 2) in (h, 3)) == by_vector]
-
-        def inter_steps(key, by_vector):
-            hh = [h for h in range(2) if (scalar_inter.get(key, 2) in (h, 3)) != by_vector]
-            if len(hh) == 2:
-                return [("inter", key, 0, HALF)]
-            return [("inter", key, h * HALF // 2, (h + 1) * HALF // 2) for h in hh]
-
         for n, pair in enumerate(pairs):
             for key in pair:
-                v_list += wide_steps(key, True)
-                s_list += wide_steps(key, False)
+                if key[0] in "xb":
+                    for planes in ((0, 1), (2, 3)):
+                        who = v_list if planes[0] // 2 in vector_widens.get(key, []) else s_list
+                        who.append(("widen", key, planes))
             for key in pair:
-                v_list += inter_steps(key, True)
-                s_list += inter_steps(key, False)
-            v_list += [("quant", key) for key in pair]
+                by_s = scalar_lays.get(key, [])
+                for who, halves in ((v_list, [h for h in range(2) if h not in by_s]), (s_list, by_s)):
+                    if len(halves) == 2:
+                        who.append(("lay", key, None))
+                    elif halves:
+                        who.append(("lay", key, halves[0]))
+            v_list += [("quantize", key) for key in pair]
             if n == 6:
-                s_list += [("cexit", 0, t) for t in range(4)]
+                s_list += [("negate",)] + [("relu", 0, t) for t in range(4)]
             if n == 6:
-                s_list += [("cexit", 1, t) for t in range(4)]
+                s_list += [("relu", 1, t) for t in range(4)]
             if n == 10:
-                s_list += [("yexit", 0, i) for i in range(4)]
-            if n == 10:
-                s_list += [("yexit", 0, i) for i in range(4, 8)]
-        v_list += [("yexit", 1, i) for i in range(8) if i in [0,1,2,3,4,5]]
-        s_list += [("yexit", 1, i) for i in range(8) if i not in [0,1,2,3,4,5]]
+                s_list += [("store", i) for i in range(TILES)]
+        v_list += [("store", n) for n in [8,10,12,14,16]]
+        s_list += [("store", n) for n in range(TILES, len(blocks)) if n not in [8,10,12,14,16]]
 
         runs = [("c", g, th, 0) for th in range(2) for g in range(G)]
         runs += [("y", g, th, nh) for nh in range(2) for th in range(2) for g in (0, 1, 2, 3, "r")]
         last_w = [int(key[1]) for pair in pairs for key in pair if key[0] == "w" and key[2] == "1"][2:]
-        ready, written = [], []
+        ready, written, passes = [], [], []
 
-        def operands(run):
-            kind, g, th, nh = run
+        def operands(kind, g, th, nh):
             if kind == "c":
                 return ["a%d" % g, "x%d%d" % (g, th)]
             return ["h%d" % th, "b%d" % nh] if g == "r" else ["x%d%d" % (g, th), "w%d%d" % (g, nh)]
 
         def can(run):
             kind, g, th, nh = run
-            if run in written or not all(key in ready for key in operands(run)):
+            if run in written or not all(key in ready for key in operands(*run)):
                 return False
             if kind == "c":
                 return True
             if nh == 0:
                 return all(r in written for r in runs if r[0] == "c" and r[2] == th)
-            return g not in last_w and all(r in written for r in runs if r[0] == "y" and r[2] == th and r[3] == 0)
+            return g not in last_w and all(r in written for r in runs if r[0] == "y" and r[2:] == (th, 0))
 
+        def emit(run, tiles):
+            kind, g, th, nh = run
+            if kind == "c":
+                passes.extend(("c", th, t, g) for t in range(4))
+            else:
+                passes.extend(("y", n, g) for n, b in enumerate(blocks) if b[0] == nh and b[1] in tiles)
+
+        split = [7] if True else []
         for pair in pairs:
             for key in pair:
                 ready.append(key)
                 for again in range(2):
                     for run in [r for r in runs if can(r)]:
                         written.append(run)
-        passes = []
-        for kind, g, th, nh in written:
-            for i in range(4):
-                passes.append(("c", g, th, i) if kind == "c" else ("y", nh, 4 * th + i, g))
-        for i in range(8):
-            for kind, g, th, nh in runs:
-                if (kind, g, th, nh) not in written and th == i // 4:
-                    passes.append(("y", nh, i, g))
-
-        def group(step):
-            return step[:1] + step[2:] if step[0] == "c" else step[:3]
-
+                        emit(run, [i for i in range(4 * run[2], 4 * run[2] + 4) if run[3] == 0 or i not in split])
+        for n, (nh, i, cols, bank) in enumerate(blocks):
+            if nh == 1:
+                for run in runs:
+                    if run[0] == "y" and run[2:] == (i // 4, 1) and ("y", n, run[1]) not in passes:
+                        passes.append(("y", n, run[1]))
         for n, step in enumerate(passes):
-            start = all(group(s) != group(step) for s in passes[:n])
-            stop = all(group(s) != group(step) for s in passes[n + 1 :])
+            start = all(s[:-1] != step[:-1] for s in passes[:n])
+            stop = all(s[:-1] != step[:-1] for s in passes[n + 1 :])
             t_list.append(step + (start, stop))
 
-        queues = {"S": s_list, "V": v_list, "T": t_list}
         all_steps = s_list + v_list + t_list
+
+        def needs(step):
+            op, args = step[0], step[1:]
+            if op == "lay":
+                key = args[0]
+                if key[0] in "xb":
+                    return [s for s in all_steps if s[0] == "widen" and s[1] == key]
+                return [s for s in all_steps if s[0] == "relu" and key == "h%d" % s[1]]
+            if op == "quantize":
+                return [s for s in all_steps if s[0] == "lay" and s[1] == args[0]]
+            if op == "c":
+                th, t, g = args[:3]
+                return [("quantize", key) for key in operands("c", g, th, 0)]
+            if op == "relu":
+                return [s for s in all_steps if s[0] == "c" and s[1:3] == args] + [("negate",)]
+            if op == "y":
+                n, g, start, stop = args
+                nh, i, cols, bank = blocks[n]
+                found = [("quantize", key) for key in operands("y", g, i // 4, nh)]
+                if start:
+                    if nh == 0:
+                        found.append(("relu", i // 4, i % 4))
+                    else:
+                        found += [("store", m) for m in range(n) if blocks[m][3] == bank]
+                return found
+            if op == "store":
+                return [s for s in all_steps if s[0] == "y" and s[1] == args[0] or s == ("store", args[0] - 1)]
+            if op == "widen" and args[0][0] == "b":
+                return [("negate",)]
+            return []
+
+        for key in ["s0","x00","a0","x10","s1","a1","x20","s2","a3","x30","s3","a2","x11","x31","x01","x21","w10","w20","vectors","w00","w30","b","w31","w21","w11","w01"]:
+            load(key)
+        queues = {"T": t_list, "V": v_list, "S": s_list}
         done = set()
-        load_small()
-        loads()
-        op_negate()
         while any(queues.values()):
             before = len(done)
             for eng in ("T", "V", "S"):

@@ -64,9 +64,16 @@ def tile_steering_directions_out_d5_kernel(tc, x_bytes, x_scale, w, a, theta, b_
 
         wide, codes, scales, grouped, banks, h_raw = {}, {}, {}, {}, {}, {}
 
+        ones = kept("ones", [P, 1], F32)
+        minus = kept("minus", [P, 1], F32)
+
+        def first_activation():
+            nc.gpsimd.memset(ones[:], 1.0)
+            nc.scalar.activation(out=minus[:], in_=ones[:], func=ACT.Copy, scale=-1.0)
+
         def op_negate(eng):
-            nc.scalar.mul(out=neg_theta[:], in_=theta_bf[:], mul=-1.0)
-            nc.scalar.mul(out=neg_b_s[:], in_=b_s[:], mul=-1.0)
+            nc.scalar.activation(out=neg_theta[:], in_=theta_bf[:], func=ACT.Copy, scale=minus[:])
+            nc.scalar.activation(out=neg_b_s[:], in_=b_s[:], func=ACT.Copy, scale=minus[:])
 
         def op_widen(eng, key, planes):
             if key not in wide:
@@ -263,6 +270,7 @@ def tile_steering_directions_out_d5_kernel(tc, x_bytes, x_scale, w, a, theta, b_
 
         for key in ["s0","x00","a0","x10","s1","a1","x20","s2","a3","x30","s3","a2","x11","x31","x01","x21","w10","w20","vectors","w00","w30","b","w31","w21","w11","w01"]:
             load(key)
+        first_activation()
         queues = {"T": t_list, "V": v_list, "S": s_list}
         done = set()
         while any(queues.values()):

from contextlib import ExitStack

import concourse.mybir as mybir

D, T, R, N = 2048, 1024, 512, 1024

F32 = mybir.dt.float32
BF16 = mybir.dt.bfloat16
U32 = mybir.dt.uint32
U8 = mybir.dt.uint8
FP8 = mybir.dt.float8_e4m3fn
FP8X4 = mybir.dt.float8_e4m3fn_x4
ACT = mybir.ActivationFunctionType
ALU = mybir.AluOpType

FLOPS = 2 * T * D * (R + N) + 2 * T * R * N

P = 128
G = D // 512
HALF = 512
TILES = T // P
RUN = 4


def tile_steering_directions_out_d5_kernel(tc, x_bytes, x_scale, w, a, theta, b_bytes, b_scale, out):
    nc = tc.nc
    with ExitStack() as ctx:
        keep = ctx.enter_context(tc.tile_pool(name="keep", bufs=1))
        stage = ctx.enter_context(tc.tile_pool(name="stage", bufs=8))
        outs = ctx.enter_context(tc.tile_pool(name="outs", bufs=8))
        psum = ctx.enter_context(tc.psum_pool(name="psum", bufs=1))
        ctx.enter_context(tc.manual_schedule())

        def kept(name, shape, dtype):
            return keep.tile(shape, dtype, name=name, align_bytes=64)

        theta_bf = kept("theta_bf", [P, 4], BF16)
        b_s = kept("b_s", [P, 4], F32)
        neg_theta = kept("neg_theta", [P, 4], F32)
        neg_b_s = kept("neg_b_s", [P, 4], F32)
        x_s, raw = {}, {}
        for g in range(G):
            x_s[g] = kept("x_s%d" % g, [P, 4], F32)

        def rows(src, g):
            return src[512 * g : 512 * (g + 1), :].rearrange("(p t) c -> p t c", t=4)

        def load(key):
            if key == "vectors":
                nc.sync.dma_start(out=theta_bf[:], in_=theta.rearrange("(p t) -> p t", t=4))
                nc.sync.dma_start(out=b_s[:], in_=rows(b_scale, 0).rearrange("p t o -> p (t o)"))
                return
            if key[0] == "s":
                g = int(key[1])
                queue = nc.scalar if g == 0 else nc.sync
                queue.dma_start(out=x_s[g][:], in_=rows(x_scale, g).rearrange("p t o -> p (t o)"))
                return
            kind, g = key[0], int(key[1]) if len(key) > 1 else 0
            src = {"a": a, "b": b_bytes, "x": x_bytes, "w": w}[kind]
            width = N if kind == "b" else HALF
            c0 = int(key[2]) * HALF if len(key) > 2 else 0
            raw[key] = kept("raw_" + key, [P, 4, width], U8 if kind in "xb" else BF16)
            nc.sync.dma_start(out=raw[key][:], in_=rows(src, g)[:, :, c0 : c0 + width])

        wide, codes, scales, grouped, banks, h_raw = {}, {}, {}, {}, {}, {}

        ones = kept("ones", [P, 1], F32)
        minus = kept("minus", [P, 1], F32)

        def first_activation():
            nc.gpsimd.memset(ones[:], 1.0)
            nc.scalar.activation(out=minus[:], in_=ones[:], func=ACT.Copy, scale=-1.0)

        def op_negate(eng):
            nc.scalar.activation(out=neg_theta[:], in_=theta_bf[:], func=ACT.Copy, scale=minus[:])
            nc.scalar.activation(out=neg_b_s[:], in_=b_s[:], func=ACT.Copy, scale=minus[:])

        def op_widen(eng, key, planes):
            if key not in wide:
                wide[key] = stage.tile([P, 4, HALF], BF16, name="wide", align_bytes=64)
            for t in planes:
                if key[0] == "x":
                    view, scale = raw[key][:, t, :], x_s[int(key[1])][:, t : t + 1]
                else:
                    c0 = int(key[1]) * HALF
                    view, scale = raw["b"][:, t, c0 : c0 + HALF], neg_b_s[:, t : t + 1]
                if eng == "S":
                    nc.scalar.activation(out=wide[key][:, t, :], in_=view.bitcast(FP8), func=ACT.Copy, scale=scale)
                else:
                    nc.vector.tensor_scalar(out=wide[key][:, t, :], in0=view.bitcast(FP8), scalar1=scale, scalar2=None, op0=ALU.mult)

        def op_lay(eng, key, half):
            if key not in grouped:
                grouped[key] = stage.tile([P, 4 * HALF], BF16, name="grouped", align_bytes=64)
            src = {"a": raw, "w": raw, "x": wide, "b": wide, "h": h_raw}[key[0]][key][:]
            if key[0] == "a":
                dst = grouped[key][:].rearrange("p (t m j) -> p m j t", t=4, j=4)
                src = src.rearrange("p j (m t) -> p m j t", t=4)
            else:
                dst = grouped[key][:].rearrange("p (c i t) -> p c t i", i=RUN, t=4)
                src = src.rearrange("p t (c i) -> p c t i", i=RUN)
            count = src.shape[1]
            part = {0: slice(0, count // 2), 1: slice(count // 2, count), None: slice(0, count)}[half]
            if eng == "V":
                nc.vector.tensor_copy(out=dst[:, part], in_=src[:, part])
            else:
                nc.scalar.copy(out=dst[:, part], in_=src[:, part])

        def op_quantize(eng, key):
            codes[key] = kept("codes_" + key, [P, HALF], U32)
            scales[key] = kept("scales_" + key, [P, HALF], U8)
            nc.vector.quantize_mx(out=codes[key][:].bitcast(FP8X4), scales=scales[key][:], in_=grouped[key][:])

        def multiply(bank, stat, block, mov, cols, start, stop):
            mine = slice(block * P, (block + 1) * P)
            nc.tensor.matmul_mx(
                out=bank[:, 0 : cols.stop - cols.start],
                lhsT=codes[stat][:, mine].bitcast(FP8X4),
                lhsT_scale=scales[stat][:, mine],
                rhs=codes[mov][:, cols].bitcast(FP8X4),
                rhs_scale=scales[mov][:, cols],
                start=start,
                stop=stop,
            )

        ALL = slice(0, HALF)
        blocks = [(nh, i, ALL, i) for nh in range(2) for i in range(TILES)]
        if True:
            blocks[-1:] = [(1, 7, slice(0, 256), 7), (1, 7, slice(256, 512), 0)]

        def new_bank(group, i):
            banks[group] = psum.tile([P, HALF], F32, name="bank%d" % i)

        def op_c(eng, th, t, g, start, stop):
            if start:
                new_bank(("c", th, t), 4 * th + t)
            multiply(banks[("c", th, t)], "a%d" % g, t, "x%d%d" % (g, th), ALL, start, stop)

        def op_relu(eng, th, t):
            if "h%d" % th not in h_raw:
                h_raw["h%d" % th] = kept("raw_h%d" % th, [P, 4, HALF], BF16)
            dst = h_raw["h%d" % th][:, t, :]
            if eng == "S":
                nc.scalar.activation(out=dst, in_=banks[("c", th, t)][:], func=ACT.Relu, bias=neg_theta[:, t : t + 1])
            else:
                nc.vector.tensor_scalar(out=dst, in0=banks[("c", th, t)][:], scalar1=neg_theta[:, t : t + 1], scalar2=0.0, op0=ALU.add, op1=ALU.max)

        def op_y(eng, n, g, start, stop):
            nh, i, cols, bank = blocks[n]
            if start:
                new_bank(("y", n), bank)
            stat, mov = ("h%d" % (i // 4), "b%d" % nh) if g == "r" else ("x%d%d" % (g, i // 4), "w%d%d" % (g, nh))
            multiply(banks[("y", n)], stat, i % 4, mov, cols, start, stop)

        def op_store(eng, n):
            nh, i, cols, bank = blocks[n]
            width = cols.stop - cols.start
            o = outs.tile([P, HALF], F32, name="o")
            if eng == "V":
                nc.vector.tensor_copy(out=o[:, 0:width], in_=banks[("y", n)][:, 0:width])
            else:
                nc.scalar.copy(out=o[:, 0:width], in_=banks[("y", n)][:, 0:width])
            nc.sync.dma_start(out=out[i * P : (i + 1) * P, nh * HALF + cols.start : nh * HALF + cols.stop], in_=o[:, 0:width])

        ops = {"negate": op_negate, "widen": op_widen, "lay": op_lay, "quantize": op_quantize, "c": op_c, "relu": op_relu, "y": op_y, "store": op_store}

        pairs = [["a0","x00"],["a1","x10"],["a3","x20"],["x30","a2"],["x11","x31"],["x01","x21"],["w10","w20"],["h0","w00"],["b0","w30"],["h1","w31"],["b1","w21"],["w11","w01"]]
        vector_widens = {"x00":[0],"x10":[0],"x21":[1],"b1":[1]}
        scalar_lays = {"x01":[1],"h1":[0],"w01":[0],"w11":[0],"w20":[0],"w21":[0],"w30":[0],"a3":[0,1]}
        v_list, s_list, t_list = [], [], []
        for n, pair in enumerate(pairs):
            for key in pair:
                if key[0] in "xb":
                    for planes in ((0, 1), (2, 3)):
                        who = v_list if planes[0] // 2 in vector_widens.get(key, []) else s_list
                        who.append(("widen", key, planes))
            for key in pair:
                by_s = scalar_lays.get(key, [])
                for who, halves in ((v_list, [h for h in range(2) if h not in by_s]), (s_list, by_s)):
                    if len(halves) == 2:
                        who.append(("lay", key, None))
                    elif halves:
                        who.append(("lay", key, halves[0]))
            v_list += [("quantize", key) for key in pair]
            if n == 6:
                s_list += [("negate",)] + [("relu", 0, t) for t in range(4)]
            if n == 6:
                s_list += [("relu", 1, t) for t in range(4)]
            if n == 10:
                s_list += [("store", i) for i in range(TILES)]
        v_list += [("store", n) for n in [8,10,12,14,16]]
        s_list += [("store", n) for n in range(TILES, len(blocks)) if n not in [8,10,12,14,16]]

        runs = [("c", g, th, 0) for th in range(2) for g in range(G)]
        runs += [("y", g, th, nh) for nh in range(2) for th in range(2) for g in (0, 1, 2, 3, "r")]
        last_w = [int(key[1]) for pair in pairs for key in pair if key[0] == "w" and key[2] == "1"][2:]
        ready, written, passes = [], [], []

        def operands(kind, g, th, nh):
            if kind == "c":
                return ["a%d" % g, "x%d%d" % (g, th)]
            return ["h%d" % th, "b%d" % nh] if g == "r" else ["x%d%d" % (g, th), "w%d%d" % (g, nh)]

        def can(run):
            kind, g, th, nh = run
            if run in written or not all(key in ready for key in operands(*run)):
                return False
            if kind == "c":
                return True
            if nh == 0:
                return all(r in written for r in runs if r[0] == "c" and r[2] == th)
            return g not in last_w and all(r in written for r in runs if r[0] == "y" and r[2:] == (th, 0))

        def emit(run, tiles):
            kind, g, th, nh = run
            if kind == "c":
                passes.extend(("c", th, t, g) for t in range(4))
            else:
                passes.extend(("y", n, g) for n, b in enumerate(blocks) if b[0] == nh and b[1] in tiles)

        split = [7] if True else []
        for pair in pairs:
            for key in pair:
                ready.append(key)
                for again in range(2):
                    for run in [r for r in runs if can(r)]:
                        written.append(run)
                        emit(run, [i for i in range(4 * run[2], 4 * run[2] + 4) if run[3] == 0 or i not in split])
        for n, (nh, i, cols, bank) in enumerate(blocks):
            if nh == 1:
                for run in runs:
                    if run[0] == "y" and run[2:] == (i // 4, 1) and ("y", n, run[1]) not in passes:
                        passes.append(("y", n, run[1]))
        for n, step in enumerate(passes):
            start = all(s[:-1] != step[:-1] for s in passes[:n])
            stop = all(s[:-1] != step[:-1] for s in passes[n + 1 :])
            t_list.append(step + (start, stop))

        all_steps = s_list + v_list + t_list

        def needs(step):
            op, args = step[0], step[1:]
            if op == "lay":
                key = args[0]
                if key[0] in "xb":
                    return [s for s in all_steps if s[0] == "widen" and s[1] == key]
                return [s for s in all_steps if s[0] == "relu" and key == "h%d" % s[1]]
            if op == "quantize":
                return [s for s in all_steps if s[0] == "lay" and s[1] == args[0]]
            if op == "c":
                th, t, g = args[:3]
                return [("quantize", key) for key in operands("c", g, th, 0)]
            if op == "relu":
                return [s for s in all_steps if s[0] == "c" and s[1:3] == args] + [("negate",)]
            if op == "y":
                n, g, start, stop = args
                nh, i, cols, bank = blocks[n]
                found = [("quantize", key) for key in operands("y", g, i // 4, nh)]
                if start:
                    if nh == 0:
                        found.append(("relu", i // 4, i % 4))
                    else:
                        found += [("store", m) for m in range(n) if blocks[m][3] == bank]
                return found
            if op == "store":
                return [s for s in all_steps if s[0] == "y" and s[1] == args[0] or s == ("store", args[0] - 1)]
            if op == "widen" and args[0][0] == "b":
                return [("negate",)]
            return []

        for key in ["s0","x00","a0","x10","s1","a1","x20","s2","a3","x30","s3","a2","x11","x31","x01","x21","w10","w20","vectors","w00","w30","b","w31","w21","w11","w01"]:
            load(key)
        first_activation()
        queues = {"T": t_list, "V": v_list, "S": s_list}
        done = set()
        while any(queues.values()):
            before = len(done)
            for eng in ("T", "V", "S"):
                while queues[eng] and all(s in done for s in needs(queues[eng][0])):
                    step = queues[eng][0]
                    queues[eng] = queues[eng][1:]
                    ops[step[0]](eng, *step[1:])
                    done.add(step)
                    if eng == "S":
                        break
            assert len(done) > before
